import numpy as np
import ml_dtypes


def mxq(x, axis, fmt="e4m3"):
    dtype, down = {"e4m3": (ml_dtypes.float8_e4m3fn, 7), "e5m2": (ml_dtypes.float8_e5m2, 14)}[fmt]
    v = np.moveaxis(np.asarray(x, np.float32).astype(ml_dtypes.bfloat16).astype(np.float64), axis, -1)
    blocks = v.reshape(v.shape[:-1] + (-1, 32))
    amax = np.abs(blocks).max(-1, keepdims=True)
    byte = np.maximum(np.where(amax > 0, np.frexp(amax)[1] - 1 + 127, 0) - down, 1)
    scale = np.exp2(byte - 127.0)
    codes = (blocks / scale).astype(np.float32).astype(dtype).astype(np.float64)
    return np.moveaxis((codes * scale).reshape(v.shape), -1, axis)


WIDE = False


def mx_kscale(k):
    if not WIDE:
        return np.ones(k)
    levels = np.array([30, -30])
    if k % 512:
        return np.exp2(np.random.permutation(np.resize(levels, k // 32))).repeat(32)
    a = np.empty((k // 512, 16))
    for p in range(k // 512):
        a[p, :8] = np.random.permutation(np.resize(levels, 8))
        for g in range(8):
            far = levels[np.abs(levels - a[p, g]) >= 10]
            a[p, g + 8] = far[np.random.randint(len(far))]
    return np.exp2(a.ravel()).repeat(32)


def f64(x):
    return np.asarray(x).astype(np.float64)


def striped(idx):
    return np.tile(np.asarray(idx).reshape(-1, 16).T, (8, 1)).astype(np.uint16)


def unstriped(offs):
    return offs[:16].T.reshape(-1).astype(np.int64)


E2M1 = np.array([0.0, 0.5, 1.0, 1.5, 2.0, 3.0, 4.0, 6.0, -0.0, -0.5, -1.0, -1.5, -2.0, -3.0, -4.0, -6.0])


def pack_weight(w, fmt):
    k, n = w.shape
    w = f64(np.asarray(w, np.float32).astype(ml_dtypes.bfloat16)).reshape(k // 32, 32, n)
    amax = np.abs(w).max(1)
    if fmt in ("e4m3", "e5m2"):
        byte = np.frexp(amax)[1] - 1 + 127 - (7 if fmt == "e4m3" else 14)
    else:
        mant, ex = np.frexp(amax / 6.0)
        byte = np.where(mant > 0.5, ex, ex - 1) + 127
    byte = np.clip(np.where(amax > 0, byte, 1), 1, 254)
    scaled = (w * np.exp2(127.0 - byte)[:, None, :]).reshape(k, n).astype(np.float32)
    by_word = np.ascontiguousarray(scaled.reshape(k // 512, 128, 4, n).transpose(0, 1, 3, 2))
    if fmt in ("e4m3", "e5m2"):
        words = by_word.astype(ml_dtypes.float8_e4m3fn if fmt == "e4m3" else ml_dtypes.float8_e5m2).view(np.uint8)
    else:
        c = by_word.astype(ml_dtypes.float4_e2m1fn).view(np.uint8) & 0xF
        words = (c[..., 0::2] | (c[..., 1::2] << 4)).reshape(k // 512, 128, 2 * n)
    return np.ascontiguousarray(words), np.ascontiguousarray(byte.astype(np.uint8).reshape(k // 512, 16, n))


def unpack_weight(words, scales, fmt):
    g, _, n = scales.shape
    words = np.ascontiguousarray(words).reshape(g, 128, n, -1)
    if fmt in ("e4m3", "e5m2"):
        vals = words.view(ml_dtypes.float8_e4m3fn if fmt == "e4m3" else ml_dtypes.float8_e5m2).astype(np.float64)
    else:
        nib = np.empty((g, 128, n, 4), np.uint8)
        nib[..., 0::2] = words & 0xF
        nib[..., 1::2] = words >> 4
        vals = E2M1[nib]
    vals = vals * np.repeat(np.exp2(scales.astype(np.float64) - 127.0), 8, axis=1)[..., None]
    return vals.transpose(0, 1, 3, 2).reshape(g * 512, n)


K, F, T, Z, J, R, C, N, L, E = 512, 512, 1024, 1024, 256, 512, 512, 256, 512, 1024


def setup_inputs():
    n = np.random.standard_normal
    idx = np.random.permutation(T)[:J]
    idx2 = np.random.permutation(Z)[:J]
    idx3 = np.random.permutation(C)[:J]
    idx4 = np.random.permutation(C)[:J]
    idx5 = np.random.permutation(E)[:J]
    fk = mx_kscale(K)
    fr = mx_kscale(R)
    ff = mx_kscale(F)
    fl = mx_kscale(L)
    xtp = pack_weight(n((K, T)) / fk[:, None], "e4m3")
    wp = pack_weight(n((K, R)) * 1 / np.sqrt(K) * fk[:, None] * fr, "e2m1")
    xop = pack_weight(n((F, Z)) / ff[:, None], "e2m1")
    w2p = pack_weight(n((F, R)) * 1 / np.sqrt(F) * ff[:, None] * fr, "e5m2")
    wbp = pack_weight(n((R, N)) * 1 / np.sqrt(R) / fr[:, None], "e5m2")
    sxp = pack_weight(n((L, J)) / fl[:, None], "e2m1")
    wsp = pack_weight(n((L, N)) * 1 / np.sqrt(L) * fl[:, None], "e5m2")
    return {
        "xt_words": xtp[0],
        "xt_scales": xtp[1],
        "w_words": wp[0],
        "w_scales": wp[1],
        "xo_words": xop[0],
        "xo_scales": xop[1],
        "w2_words": w2p[0],
        "w2_scales": w2p[1],
        "wb_words": wbp[0],
        "wb_scales": wbp[1],
        "sx_words": sxp[0],
        "sx_scales": sxp[1],
        "ws_words": wsp[0],
        "ws_scales": wsp[1],
        "offs": striped(idx),
        "offs2": striped(idx2),
        "offs3": striped(idx3),
        "offs4": striped(idx4),
        "offs5": striped(idx5),
    }


def reference(xt_words, xt_scales, w_words, w_scales, xo_words, xo_scales, w2_words, w2_scales, wb_words, wb_scales, sx_words, sx_scales, ws_words, ws_scales, offs, offs2, offs3, offs4, offs5):
    idx = unstriped(offs)
    idx2 = unstriped(offs2)
    idx3 = unstriped(offs3)
    idx4 = unstriped(offs4)
    idx5 = unstriped(offs5)
    xtu = unpack_weight(xt_words, xt_scales, "e4m3")
    wu = unpack_weight(w_words, w_scales, "e2m1")
    xou = unpack_weight(xo_words, xo_scales, "e2m1")
    w2u = unpack_weight(w2_words, w2_scales, "e5m2")
    wbu = unpack_weight(wb_words, wb_scales, "e5m2")
    sxu = unpack_weight(sx_words, sx_scales, "e2m1")
    wsu = unpack_weight(ws_words, ws_scales, "e5m2")
    xtidxg = xtu[:, idx]
    a = wu.T @ xtidxg
    xoidx2g = xou[:, idx2]
    b = w2u.T @ xoidx2g
    pw = np.zeros((R, C))
    pw[:, idx3] = a
    hid = np.abs(pw[:, idx4] - b)
    hidq = mxq(hid, 0, "e4m3")
    p = wbu.T @ hidq + wsu.T @ sxu
    y = np.zeros((N, E))
    y[:, idx5] = p
    return y

@@ -1,0 +1,185 @@
+from contextlib import ExitStack
+
+import concourse.mybir as mybir
+
+K, F, T, Z, J, R, C, N, L, E = 512, 512, 1024, 1024, 256, 512, 512, 256, 512, 1024
+FLOPS = 2 * J * (K * R + F * R + R * N + L * N)
+
+F32 = mybir.dt.float32
+BF16 = mybir.dt.bfloat16
+I32 = mybir.dt.int32
+U32 = mybir.dt.uint32
+U16 = mybir.dt.uint16
+U8 = mybir.dt.uint8
+E4M3 = mybir.dt.float8_e4m3fn_x4
+E5M2 = mybir.dt.float8_e5m2_x4
+E2M1 = mybir.dt.float4_e2m1fn_x4
+ACT = mybir.ActivationFunctionType
+ALU = mybir.AluOpType
+
+P = 128
+PACK = 4
+
+
+def tile_list_twotab_board_skip_scattered_kernel(
+    tc, xt_words, xt_scales, w_words, w_scales, xo_words, xo_scales, w2_words, w2_scales,
+    wb_words, wb_scales, sx_words, sx_scales, ws_words, ws_scales,
+    offs, offs2, offs3, offs4, offs5, out,
+):
+    nc = tc.nc
+    with ExitStack() as ctx:
+        lists = ctx.enter_context(tc.tile_pool(name="lists", bufs=1))
+        keep = ctx.enter_context(tc.tile_pool(name="keep", bufs=1))
+        psum = ctx.enter_context(tc.psum_pool(name="psum", bufs=1))
+
+        def load_list(name, src):
+            tile = lists.tile([P, J // 16], U16, name=name)
+            nc.sync.dma_start(tile[:], src)
+            return tile
+
+        def load_words(queue, name, src, width, dtype):
+            tile = keep.tile([P, width], dtype, name=name, align_bytes=64)
+            rows = src[0]
+            if rows.ndim == 3:
+                rows = rows.rearrange("p n t -> p (n t)")
+            queue.dma_start(tile[:].bitcast(I32), rows.bitcast(I32))
+            return tile
+
+        def clear_scales(name, width):
+            tile = keep.tile([P, width], U8, name=name, align_bytes=64)
+            nc.vector.memset(tile[:].bitcast(I32), 0)
+            return tile
+
+        def load_scales(queue, plane, src):
+            rows = src[0].bitcast(I32)
+            for q in range(4):
+                queue.dma_start(plane[32 * q : 32 * q + 4, :].bitcast(I32), rows[4 * q : 4 * q + 4, :])
+
+        def deal_columns(name, src, dtype):
+            tile = keep.tile([P, PACK, P], dtype, name=name, align_bytes=64)
+            nc.gpsimd.tensor_copy(out=tile[:], in_=src.rearrange("p (m t) -> p t m", t=PACK))
+            return tile
+
+        def gather(name, window, offsets, dtype):
+            tile = keep.tile([P, J], dtype, name=name, align_bytes=64)
+            nc.vector.tensor_copy(out=tile[:], in_=window[:].indirect(offsets[:]))
+            return tile
+
+        w_s = clear_scales("w_s", R)
+        xt_s = clear_scales("xt_s", T)
+        xo_s = clear_scales("xo_s", Z)
+        rest_s = clear_scales("rest_s", R + N + J + N)
+        w2_s, ws_s, sx_s, wb_s = rest_s[:, 0:R], rest_s[:, R : R + N], rest_s[:, R + N : R + N + J], rest_s[:, R + N + J :]
+
+        idx = load_list("idx", offs)
+        xt_w = load_words(nc.sync, "xt_w", xt_words, T, U32)
+        w_w = load_words(nc.sync, "w_w", w_words, R, U16)
+        load_scales(nc.scalar, w_s, w_scales)
+        idx2 = load_list("idx2", offs2)
+        load_scales(nc.sync, xt_s, xt_scales)
+        xo_w = load_words(nc.sync, "xo_w", xo_words, Z, U16)
+        idx3 = load_list("idx3", offs3)
+        load_scales(nc.sync, xo_s, xo_scales)
+        w2_w = load_words(nc.sync, "w2_w", w2_words, R, U32)
+        load_scales(nc.sync, w2_s, w2_scales)
+        idx4 = load_list("idx4", offs4)
+        ws_w = load_words(nc.sync, "ws_w", ws_words, N, U32)
+        load_scales(nc.sync, ws_s, ws_scales)
+        sx_w = load_words(nc.sync, "sx_w", sx_words, J, U16)
+        load_scales(nc.sync, sx_s, sx_scales)
+        wb_w = load_words(nc.sync, "wb_w", wb_words, N, U32)
+        load_scales(nc.sync, wb_s, wb_scales)
+        idx5 = load_list("idx5", offs5)
+
+        boards = [keep.tile([P, C], F32, name="board%d" % t) for t in range(PACK)]
+        pages = [keep.tile([P, E], F32, name="page%d" % h) for h in range(N // P)]
+        for tile in boards + pages:
+            nc.vector.memset(tile[:], 0.0)
+
+        w_wd = keep.tile([P, PACK, P], U16, name="w_wd", align_bytes=64)
+        nc.gpsimd.tensor_copy(
+            out=w_wd[:].bitcast(U8).rearrange("p t (m b) -> p t m b", b=2),
+            in_=w_w[:].bitcast(U8).rearrange("p (m t b) -> p t m b", t=PACK, b=2),
+        )
+        w_sd = deal_columns("w_sd", w_s[:], U8)
+        xg_w = gather("xg_w", xt_w, idx, U32)
+        xg_s = gather("xg_s", xt_s, idx, U8)
+
+        a_ps = [psum.tile([P, J], F32, name="a_ps%d" % t, tag="bank%d" % t) for t in range(PACK)]
+        for t in range(PACK):
+            nc.tensor.matmul_mx(
+                out=a_ps[t][:], lhsT=w_wd[:, t, :].bitcast(E2M1), lhsT_scale=w_sd[:, t, :],
+                rhs=xg_w[:].bitcast(E4M3), rhs_scale=xg_s[:], start=True, stop=True,
+            )
+        a_sb = [keep.tile([P, J], F32, name="a_sb%d" % t) for t in range(PACK)]
+        for t in (1, 0, 3, 2):
+            nc.scalar.activation(out=a_sb[t][:], in_=a_ps[t][:], func=ACT.Copy)
+
+        og_w = gather("og_w", xo_w, idx2, U16)
+        og_s = gather("og_s", xo_s, idx2, U8)
+        w2_wd = deal_columns("w2_wd", w2_w[:], U32)
+        w2_sd = deal_columns("w2_sd", w2_s, U8)
+
+        halves = [slice(h * P, (h + 1) * P) for h in range(2)]
+        b_ps = [psum.tile([P, PACK, P], F32, name="b_ps%d" % h, tag="bank%d" % (4 + h)) for h in range(2)]
+        for h in range(2):
+            for t in range(PACK):
+                nc.tensor.matmul_mx(
+                    out=b_ps[h][:, t, :], lhsT=w2_wd[:, t, :].bitcast(E5M2), lhsT_scale=w2_sd[:, t, :],
+                    rhs=og_w[:, halves[h]].bitcast(E2M1), rhs_scale=og_s[:, halves[h]], start=True, stop=True,
+                )
+
+        p_ps = {}
+        for h in range(2):
+            for g in range(2):
+                p_ps[h, g] = psum.tile([P, P], F32, name="p_ps%d%d" % (h, g), tag="bank%d" % ((6 + 2 * h + g) % 8))
+                nc.tensor.matmul_mx(
+                    out=p_ps[h, g][:], lhsT=ws_w[:, halves[g]].bitcast(E5M2), lhsT_scale=ws_s[:, halves[g]],
+                    rhs=sx_w[:, halves[h]].bitcast(E2M1), rhs_scale=sx_s[:, halves[h]], start=True, stop=False,
+                )
+
+        for t in range(PACK):
+            if t % 2 == 0:
+                nc.scalar.activation(out=boards[t][:].indirect(idx3[:]), in_=a_sb[t][:], func=ACT.Copy)
+            else:
+                nc.vector.tensor_copy(out=boards[t][:].indirect(idx3[:]), in_=a_sb[t][:])
+
+        picked = keep.tile([P, PACK, J], F32, name="picked")
+        for t in (1, 3):
+            nc.vector.tensor_copy(out=picked[:, t, :], in_=boards[t][:].indirect(idx4[:]))
+        for h in range(2):
+            for t in (0, 2):
+                nc.scalar.activation(
+                    out=picked[:, t, halves[h]], in_=boards[t][:].indirect(idx4[:, 8 * h : 8 * h + 8]), func=ACT.Copy
+                )
+
+        diff = [keep.tile([P, PACK, P], F32, name="diff%d" % h) for h in range(2)]
+        hid = [keep.tile([P, P, PACK], BF16, name="hid%d" % h, align_bytes=64) for h in range(2)]
+        hq_w = [keep.tile([P, P], U32, name="hq_w%d" % h, align_bytes=64) for h in range(2)]
+        hq_s = [keep.tile([P, P], U8, name="hq_s%d" % h, align_bytes=64) for h in range(2)]
+        for h in range(2):
+            nc.vector.tensor_tensor(out=diff[h][:], in0=picked[:, :, halves[h]], in1=b_ps[h][:], op=ALU.subtract)
+        for h in range(2):
+            nc.scalar.activation(
+                out=hid[h][:].rearrange("p (c i) t -> p c t i", i=4),
+                in_=diff[h][:].rearrange("p t (c i) -> p c t i", i=4),
+                func=ACT.Abs,
+            )
+            nc.vector.quantize_mx(
+                out=hq_w[h][:].bitcast(E4M3), scales=hq_s[h][:], in_=hid[h][:].rearrange("p j t -> p (j t)")
+            )
+            for g in range(2):
+                nc.tensor.matmul_mx(
+                    out=p_ps[h, g][:], lhsT=wb_w[:, halves[g]].bitcast(E5M2), lhsT_scale=wb_s[:, halves[g]],
+                    rhs=hq_w[h][:].bitcast(E4M3), rhs_scale=hq_s[h][:], start=False, stop=True,
+                )
+
+        for h in range(2):
+            p_sb = [keep.tile([P, P], F32, name="p_sb%d%d" % (h, g)) for g in range(2)]
+            places = idx5[:, 8 * h : 8 * h + 8]
+            nc.scalar.activation(out=p_sb[0][:], in_=p_ps[h, 0][:], func=ACT.Copy)
+            nc.scalar.activation(out=pages[0][:].indirect(places), in_=p_sb[0][:], func=ACT.Copy)
+            nc.vector.tensor_copy(out=p_sb[1][:], in_=p_ps[h, 1][:])
+            nc.vector.tensor_copy(out=pages[1][:].indirect(places), in_=p_sb[1][:])
+        nc.sync.dma_start(out[0:P, :], pages[0][:])
+        nc.sync.dma_start(out[P : 2 * P, :], pages[1][:])

@@ -38,7 +38,7 @@ def tile_list_twotab_board_skip_scattered_kernel(
             return tile
 
         def load_words(queue, name, src, width, dtype):
-            tile = keep.tile([P, width], dtype, name=name, align_bytes=64)
+            tile = keep.tile([P, width], dtype, name=name, tag=name, align_bytes=64)
             rows = src[0]
             if rows.ndim == 3:
                 rows = rows.rearrange("p n t -> p (n t)")
@@ -46,18 +46,26 @@ def tile_list_twotab_board_skip_scattered_kernel(
             return tile
 
         def clear_scales(name, width):
-            tile = keep.tile([P, width], U8, name=name, align_bytes=64)
+            tile = keep.tile([P, width], U8, name=name, tag=name, align_bytes=64)
             nc.vector.memset(tile[:].bitcast(I32), 0)
             return tile
 
-        def load_scales(queue, plane, src):
+        def load_scales(queue, plane, src, quadrants=range(4)):
             rows = src[0].bitcast(I32)
-            for q in range(4):
+            for q in quadrants:
                 queue.dma_start(plane[32 * q : 32 * q + 4, :].bitcast(I32), rows[4 * q : 4 * q + 4, :])
 
-        def deal_columns(name, src, dtype):
+        def load_scales_repeated(plane, src, quadrants):
+            rows = src[0].bitcast(I32).rearrange("(q r) c -> q r c", r=4)
+            for q in quadrants:
+                nc.sync.dma_start(
+                    plane[32 * q : 32 * (q + 1), :].bitcast(I32),
+                    rows[q : q + 1].to_broadcast([8, 4, rows.shape[2]]),
+                )
+
+        def deal_columns(engine, name, src, dtype):
             tile = keep.tile([P, PACK, P], dtype, name=name, align_bytes=64)
-            nc.gpsimd.tensor_copy(out=tile[:], in_=src.rearrange("p (m t) -> p t m", t=PACK))
+            engine.tensor_copy(out=tile[:], in_=src.rearrange("p (m t) -> p t m", t=PACK))
             return tile
 
         def gather(name, window, offsets, dtype):
@@ -65,60 +73,61 @@ def tile_list_twotab_board_skip_scattered_kernel(
             nc.vector.tensor_copy(out=tile[:], in_=window[:].indirect(offsets[:]))
             return tile
 
-        w_s = clear_scales("w_s", R)
-        xt_s = clear_scales("xt_s", T)
+        xt_s = keep.tile([P, T], U8, name="xt_s", align_bytes=64)
+        w_s = keep.tile([P, R], U8, name="w_s", tag="w_s", align_bytes=64)
         xo_s = clear_scales("xo_s", Z)
         rest_s = clear_scales("rest_s", R + N + J + N)
         w2_s, ws_s, sx_s, wb_s = rest_s[:, 0:R], rest_s[:, R : R + N], rest_s[:, R + N : R + N + J], rest_s[:, R + N + J :]
 
         idx = load_list("idx", offs)
-        xt_w = load_words(nc.sync, "xt_w", xt_words, T, U32)
+        load_scales_repeated(xt_s, xt_scales, range(4))
+        load_scales_repeated(w_s, w_scales, range(0, 1))
         w_w = load_words(nc.sync, "w_w", w_words, R, U16)
-        load_scales(nc.scalar, w_s, w_scales)
+        xt_w = load_words(nc.sync, "xt_w", xt_words, T, U32)
+        load_scales_repeated(w_s, w_scales, range(1, 4))
         idx2 = load_list("idx2", offs2)
-        load_scales(nc.sync, xt_s, xt_scales)
         xo_w = load_words(nc.sync, "xo_w", xo_words, Z, U16)
+        load_scales(nc.sync, xo_s, xo_scales, range(0, 1))
         idx3 = load_list("idx3", offs3)
-        load_scales(nc.sync, xo_s, xo_scales)
+        load_scales(nc.sync, xo_s, xo_scales, range(1, 4))
         w2_w = load_words(nc.sync, "w2_w", w2_words, R, U32)
         load_scales(nc.sync, w2_s, w2_scales)
         idx4 = load_list("idx4", offs4)
         ws_w = load_words(nc.sync, "ws_w", ws_words, N, U32)
-        load_scales(nc.sync, ws_s, ws_scales)
         sx_w = load_words(nc.sync, "sx_w", sx_words, J, U16)
-        load_scales(nc.sync, sx_s, sx_scales)
         wb_w = load_words(nc.sync, "wb_w", wb_words, N, U32)
+        load_scales(nc.sync, ws_s, ws_scales)
+        load_scales(nc.sync, sx_s, sx_scales)
         load_scales(nc.sync, wb_s, wb_scales)
         idx5 = load_list("idx5", offs5)
 
         boards = [keep.tile([P, C], F32, name="board%d" % t) for t in range(PACK)]
-        pages = [keep.tile([P, E], F32, name="page%d" % h) for h in range(N // P)]
-        for tile in boards + pages:
+        page0 = keep.tile([P, E], F32, name="page0")
+        page1 = keep.tile([P, E], F32, name="page1")
+        for tile in boards + [page0, page1]:
             nc.vector.memset(tile[:], 0.0)
 
-        w_wd = keep.tile([P, PACK, P], U16, name="w_wd", align_bytes=64)
-        nc.gpsimd.tensor_copy(
-            out=w_wd[:].bitcast(U8).rearrange("p t (m b) -> p t m b", b=2),
-            in_=w_w[:].bitcast(U8).rearrange("p (m t b) -> p t m b", t=PACK, b=2),
-        )
-        w_sd = deal_columns("w_sd", w_s[:], U8)
-        xg_w = gather("xg_w", xt_w, idx, U32)
         xg_s = gather("xg_s", xt_s, idx, U8)
+        w_wd = deal_columns(nc.vector, "w_wd", w_w[:], U16)
+        xg_w = gather("xg_w", xt_w, idx, U32)
+        w_sd = deal_columns(nc.vector, "w_sd", w_s[:], U8)
+
+        og_w = gather("og_w", xo_w, idx2, U16)
 
         a_ps = [psum.tile([P, J], F32, name="a_ps%d" % t, tag="bank%d" % t) for t in range(PACK)]
-        for t in range(PACK):
+        for t in (1, 0, 2, 3):
             nc.tensor.matmul_mx(
                 out=a_ps[t][:], lhsT=w_wd[:, t, :].bitcast(E2M1), lhsT_scale=w_sd[:, t, :],
                 rhs=xg_w[:].bitcast(E4M3), rhs_scale=xg_s[:], start=True, stop=True,
             )
         a_sb = [keep.tile([P, J], F32, name="a_sb%d" % t) for t in range(PACK)]
-        for t in (1, 0, 3, 2):
+        for t in (1, 0, 2, 3):
             nc.scalar.activation(out=a_sb[t][:], in_=a_ps[t][:], func=ACT.Copy)
+        nc.vector.tensor_copy(out=boards[1][:].indirect(idx3[:]), in_=a_sb[1][:])
 
-        og_w = gather("og_w", xo_w, idx2, U16)
         og_s = gather("og_s", xo_s, idx2, U8)
-        w2_wd = deal_columns("w2_wd", w2_w[:], U32)
-        w2_sd = deal_columns("w2_sd", w2_s, U8)
+        w2_wd = deal_columns(nc.gpsimd, "w2_wd", w2_w[:], U32)
+        w2_sd = deal_columns(nc.gpsimd, "w2_sd", w2_s, U8)
 
         halves = [slice(h * P, (h + 1) * P) for h in range(2)]
         b_ps = [psum.tile([P, PACK, P], F32, name="b_ps%d" % h, tag="bank%d" % (4 + h)) for h in range(2)]
@@ -129,36 +138,32 @@ def tile_list_twotab_board_skip_scattered_kernel(
                     rhs=og_w[:, halves[h]].bitcast(E2M1), rhs_scale=og_s[:, halves[h]], start=True, stop=True,
                 )
 
+        for t in (0, 2):
+            nc.scalar.activation(out=boards[t][:].indirect(idx3[:]), in_=a_sb[t][:], func=ACT.Copy)
+        nc.vector.tensor_copy(out=boards[3][:].indirect(idx3[:]), in_=a_sb[3][:])
+
+        picked = keep.tile([P, PACK, J], F32, name="picked")
+        for h, t in ((0, 1), (0, 3), (1, 1)):
+            nc.vector.tensor_copy(out=picked[:, t, halves[h]], in_=boards[t][:].indirect(idx4[:, 8 * h : 8 * h + 8]))
+        for h, t in ((0, 0), (0, 2), (1, 0), (1, 2), (1, 3)):
+            nc.scalar.activation(
+                out=picked[:, t, halves[h]], in_=boards[t][:].indirect(idx4[:, 8 * h : 8 * h + 8]), func=ACT.Copy
+            )
+
+        diff = [keep.tile([P, PACK, P], F32, name="diff%d" % h) for h in range(2)]
+        hid = [keep.tile([P, P, PACK], BF16, name="hid%d" % h, tag="hid%d" % h, align_bytes=64) for h in range(2)]
+        hq_w = [keep.tile([P, P], U32, name="hq_w%d" % h, align_bytes=64) for h in range(2)]
+        hq_s = [keep.tile([P, P], U8, name="hq_s%d" % h, align_bytes=64) for h in range(2)]
+        nc.vector.tensor_tensor(out=diff[0][:], in0=picked[:, :, halves[0]], in1=b_ps[0][:], op=ALU.subtract)
+        nc.vector.tensor_tensor(out=diff[1][:], in0=picked[:, :, halves[1]], in1=b_ps[1][:], op=ALU.subtract)
         p_ps = {}
         for h in range(2):
             for g in range(2):
-                p_ps[h, g] = psum.tile([P, P], F32, name="p_ps%d%d" % (h, g), tag="bank%d" % ((6 + 2 * h + g) % 8))
+                p_ps[h, g] = psum.tile([P, P], F32, name="p_ps%d%d" % (h, g), tag="bank%d" % (2 * h + g))
                 nc.tensor.matmul_mx(
                     out=p_ps[h, g][:], lhsT=ws_w[:, halves[g]].bitcast(E5M2), lhsT_scale=ws_s[:, halves[g]],
                     rhs=sx_w[:, halves[h]].bitcast(E2M1), rhs_scale=sx_s[:, halves[h]], start=True, stop=False,
                 )
-
-        for t in range(PACK):
-            if t % 2 == 0:
-                nc.scalar.activation(out=boards[t][:].indirect(idx3[:]), in_=a_sb[t][:], func=ACT.Copy)
-            else:
-                nc.vector.tensor_copy(out=boards[t][:].indirect(idx3[:]), in_=a_sb[t][:])
-
-        picked = keep.tile([P, PACK, J], F32, name="picked")
-        for t in (1, 3):
-            nc.vector.tensor_copy(out=picked[:, t, :], in_=boards[t][:].indirect(idx4[:]))
-        for h in range(2):
-            for t in (0, 2):
-                nc.scalar.activation(
-                    out=picked[:, t, halves[h]], in_=boards[t][:].indirect(idx4[:, 8 * h : 8 * h + 8]), func=ACT.Copy
-                )
-
-        diff = [keep.tile([P, PACK, P], F32, name="diff%d" % h) for h in range(2)]
-        hid = [keep.tile([P, P, PACK], BF16, name="hid%d" % h, align_bytes=64) for h in range(2)]
-        hq_w = [keep.tile([P, P], U32, name="hq_w%d" % h, align_bytes=64) for h in range(2)]
-        hq_s = [keep.tile([P, P], U8, name="hq_s%d" % h, align_bytes=64) for h in range(2)]
-        for h in range(2):
-            nc.vector.tensor_tensor(out=diff[h][:], in0=picked[:, :, halves[h]], in1=b_ps[h][:], op=ALU.subtract)
         for h in range(2):
             nc.scalar.activation(
                 out=hid[h][:].rearrange("p (c i) t -> p c t i", i=4),
@@ -174,12 +179,14 @@ def tile_list_twotab_board_skip_scattered_kernel(
                     rhs=hq_w[h][:].bitcast(E4M3), rhs_scale=hq_s[h][:], start=False, stop=True,
                 )
 
-        for h in range(2):
-            p_sb = [keep.tile([P, P], F32, name="p_sb%d%d" % (h, g)) for g in range(2)]
-            places = idx5[:, 8 * h : 8 * h + 8]
-            nc.scalar.activation(out=p_sb[0][:], in_=p_ps[h, 0][:], func=ACT.Copy)
-            nc.scalar.activation(out=pages[0][:].indirect(places), in_=p_sb[0][:], func=ACT.Copy)
-            nc.vector.tensor_copy(out=p_sb[1][:], in_=p_ps[h, 1][:])
-            nc.vector.tensor_copy(out=pages[1][:].indirect(places), in_=p_sb[1][:])
-        nc.sync.dma_start(out[0:P, :], pages[0][:])
-        nc.sync.dma_start(out[P : 2 * P, :], pages[1][:])
+        p0_sb = keep.tile([P, J], F32, name="p0_sb")
+        p1_sb = keep.tile([P, J], F32, name="p1_sb", tag="hid1", align_bytes=64)
+        nc.scalar.activation(out=p0_sb[:, halves[0]], in_=p_ps[0, 0][:], func=ACT.Copy)
+        nc.scalar.activation(out=page0[:].indirect(idx5[:, 0:8]), in_=p0_sb[:, halves[0]], func=ACT.Copy)
+        nc.vector.tensor_copy(out=p1_sb[:, halves[0]], in_=p_ps[0, 1][:])
+        nc.vector.tensor_copy(out=p0_sb[:, halves[1]], in_=p_ps[1, 0][:])
+        nc.vector.tensor_copy(out=p1_sb[:, halves[1]], in_=p_ps[1, 1][:])
+        nc.scalar.activation(out=page0[:].indirect(idx5[:, 8:16]), in_=p0_sb[:, halves[1]], func=ACT.Copy)
+        nc.vector.tensor_copy(out=page1[:].indirect(idx5[:]), in_=p1_sb[:])
+        nc.sync.dma_start(out[0:P, :], page0[:])
+        nc.sync.dma_start(out[P : 2 * P, :], page1[:])

from contextlib import ExitStack

import concourse.mybir as mybir

K, F, T, Z, J, R, C, N, L, E = 512, 512, 1024, 1024, 256, 512, 512, 256, 512, 1024
FLOPS = 2 * J * (K * R + F * R + R * N + L * N)

F32 = mybir.dt.float32
BF16 = mybir.dt.bfloat16
I32 = mybir.dt.int32
U32 = mybir.dt.uint32
U16 = mybir.dt.uint16
U8 = mybir.dt.uint8
E4M3 = mybir.dt.float8_e4m3fn_x4
E5M2 = mybir.dt.float8_e5m2_x4
E2M1 = mybir.dt.float4_e2m1fn_x4
ACT = mybir.ActivationFunctionType
ALU = mybir.AluOpType

P = 128
PACK = 4


def tile_list_twotab_board_skip_scattered_kernel(
    tc, xt_words, xt_scales, w_words, w_scales, xo_words, xo_scales, w2_words, w2_scales,
    wb_words, wb_scales, sx_words, sx_scales, ws_words, ws_scales,
    offs, offs2, offs3, offs4, offs5, out,
):
    nc = tc.nc
    with ExitStack() as ctx:
        lists = ctx.enter_context(tc.tile_pool(name="lists", bufs=1))
        keep = ctx.enter_context(tc.tile_pool(name="keep", bufs=1))
        psum = ctx.enter_context(tc.psum_pool(name="psum", bufs=1))

        def load_list(name, src):
            tile = lists.tile([P, J // 16], U16, name=name)
            nc.sync.dma_start(tile[:], src)
            return tile

        def load_words(queue, name, src, width, dtype):
            tile = keep.tile([P, width], dtype, name=name, tag=name, align_bytes=64)
            rows = src[0]
            if rows.ndim == 3:
                rows = rows.rearrange("p n t -> p (n t)")
            queue.dma_start(tile[:].bitcast(I32), rows.bitcast(I32))
            return tile

        def clear_scales(name, width):
            tile = keep.tile([P, width], U8, name=name, tag=name, align_bytes=64)
            nc.vector.memset(tile[:].bitcast(I32), 0)
            return tile

        def load_scales(queue, plane, src, quadrants=range(4)):
            rows = src[0].bitcast(I32)
            for q in quadrants:
                queue.dma_start(plane[32 * q : 32 * q + 4, :].bitcast(I32), rows[4 * q : 4 * q + 4, :])

        def load_scales_repeated(plane, src, quadrants):
            rows = src[0].bitcast(I32).rearrange("(q r) c -> q r c", r=4)
            for q in quadrants:
                nc.sync.dma_start(
                    plane[32 * q : 32 * (q + 1), :].bitcast(I32),
                    rows[q : q + 1].to_broadcast([8, 4, rows.shape[2]]),
                )

        def deal_columns(engine, name, src, dtype):
            tile = keep.tile([P, PACK, P], dtype, name=name, align_bytes=64)
            engine.tensor_copy(out=tile[:], in_=src.rearrange("p (m t) -> p t m", t=PACK))
            return tile

        def gather(name, window, offsets, dtype):
            tile = keep.tile([P, J], dtype, name=name, align_bytes=64)
            nc.vector.tensor_copy(out=tile[:], in_=window[:].indirect(offsets[:]))
            return tile

        xt_s = keep.tile([P, T], U8, name="xt_s", align_bytes=64)
        w_s = keep.tile([P, R], U8, name="w_s", tag="w_s", align_bytes=64)
        xo_s = clear_scales("xo_s", Z)
        rest_s = clear_scales("rest_s", R + N + J + N)
        w2_s, ws_s, sx_s, wb_s = rest_s[:, 0:R], rest_s[:, R : R + N], rest_s[:, R + N : R + N + J], rest_s[:, R + N + J :]

        idx = load_list("idx", offs)
        load_scales_repeated(xt_s, xt_scales, range(4))
        load_scales_repeated(w_s, w_scales, range(0, 1))
        w_w = load_words(nc.sync, "w_w", w_words, R, U16)
        xt_w = load_words(nc.sync, "xt_w", xt_words, T, U32)
        load_scales_repeated(w_s, w_scales, range(1, 4))
        idx2 = load_list("idx2", offs2)
        xo_w = load_words(nc.sync, "xo_w", xo_words, Z, U16)
        load_scales(nc.sync, xo_s, xo_scales, range(0, 1))
        idx3 = load_list("idx3", offs3)
        load_scales(nc.sync, xo_s, xo_scales, range(1, 4))
        w2_w = load_words(nc.sync, "w2_w", w2_words, R, U32)
        load_scales(nc.sync, w2_s, w2_scales)
        idx4 = load_list("idx4", offs4)
        ws_w = load_words(nc.sync, "ws_w", ws_words, N, U32)
        sx_w = load_words(nc.sync, "sx_w", sx_words, J, U16)
        wb_w = load_words(nc.sync, "wb_w", wb_words, N, U32)
        load_scales(nc.sync, ws_s, ws_scales)
        load_scales(nc.sync, sx_s, sx_scales)
        load_scales(nc.sync, wb_s, wb_scales)
        idx5 = load_list("idx5", offs5)

        boards = [keep.tile([P, C], F32, name="board%d" % t) for t in range(PACK)]
        page0 = keep.tile([P, E], F32, name="page0")
        page1 = keep.tile([P, E], F32, name="page1")
        for tile in boards + [page0, page1]:
            nc.vector.memset(tile[:], 0.0)

        xg_s = gather("xg_s", xt_s, idx, U8)
        w_wd = deal_columns(nc.vector, "w_wd", w_w[:], U16)
        xg_w = gather("xg_w", xt_w, idx, U32)
        w_sd = deal_columns(nc.vector, "w_sd", w_s[:], U8)

        og_w = gather("og_w", xo_w, idx2, U16)

        a_ps = [psum.tile([P, J], F32, name="a_ps%d" % t, tag="bank%d" % t) for t in range(PACK)]
        for t in (1, 0, 2, 3):
            nc.tensor.matmul_mx(
                out=a_ps[t][:], lhsT=w_wd[:, t, :].bitcast(E2M1), lhsT_scale=w_sd[:, t, :],
                rhs=xg_w[:].bitcast(E4M3), rhs_scale=xg_s[:], start=True, stop=True,
            )
        a_sb = [keep.tile([P, J], F32, name="a_sb%d" % t) for t in range(PACK)]
        for t in (1, 0, 2, 3):
            nc.scalar.activation(out=a_sb[t][:], in_=a_ps[t][:], func=ACT.Copy)
        nc.vector.tensor_copy(out=boards[1][:].indirect(idx3[:]), in_=a_sb[1][:])

        og_s = gather("og_s", xo_s, idx2, U8)
        w2_wd = deal_columns(nc.gpsimd, "w2_wd", w2_w[:], U32)
        w2_sd = deal_columns(nc.gpsimd, "w2_sd", w2_s, U8)

        halves = [slice(h * P, (h + 1) * P) for h in range(2)]
        b_ps = [psum.tile([P, PACK, P], F32, name="b_ps%d" % h, tag="bank%d" % (4 + h)) for h in range(2)]
        for h in range(2):
            for t in range(PACK):
                nc.tensor.matmul_mx(
                    out=b_ps[h][:, t, :], lhsT=w2_wd[:, t, :].bitcast(E5M2), lhsT_scale=w2_sd[:, t, :],
                    rhs=og_w[:, halves[h]].bitcast(E2M1), rhs_scale=og_s[:, halves[h]], start=True, stop=True,
                )

        for t in (0, 2):
            nc.scalar.activation(out=boards[t][:].indirect(idx3[:]), in_=a_sb[t][:], func=ACT.Copy)
        nc.vector.tensor_copy(out=boards[3][:].indirect(idx3[:]), in_=a_sb[3][:])

        picked = keep.tile([P, PACK, J], F32, name="picked")
        for h, t in ((0, 1), (0, 3), (1, 1)):
            nc.vector.tensor_copy(out=picked[:, t, halves[h]], in_=boards[t][:].indirect(idx4[:, 8 * h : 8 * h + 8]))
        for h, t in ((0, 0), (0, 2), (1, 0), (1, 2), (1, 3)):
            nc.scalar.activation(
                out=picked[:, t, halves[h]], in_=boards[t][:].indirect(idx4[:, 8 * h : 8 * h + 8]), func=ACT.Copy
            )

        diff = [keep.tile([P, PACK, P], F32, name="diff%d" % h) for h in range(2)]
        hid = [keep.tile([P, P, PACK], BF16, name="hid%d" % h, tag="hid%d" % h, align_bytes=64) for h in range(2)]
        hq_w = [keep.tile([P, P], U32, name="hq_w%d" % h, align_bytes=64) for h in range(2)]
        hq_s = [keep.tile([P, P], U8, name="hq_s%d" % h, align_bytes=64) for h in range(2)]
        nc.vector.tensor_tensor(out=diff[0][:], in0=picked[:, :, halves[0]], in1=b_ps[0][:], op=ALU.subtract)
        nc.vector.tensor_tensor(out=diff[1][:], in0=picked[:, :, halves[1]], in1=b_ps[1][:], op=ALU.subtract)
        p_ps = {}
        for h in range(2):
            for g in range(2):
                p_ps[h, g] = psum.tile([P, P], F32, name="p_ps%d%d" % (h, g), tag="bank%d" % (2 * h + g))
                nc.tensor.matmul_mx(
                    out=p_ps[h, g][:], lhsT=ws_w[:, halves[g]].bitcast(E5M2), lhsT_scale=ws_s[:, halves[g]],
                    rhs=sx_w[:, halves[h]].bitcast(E2M1), rhs_scale=sx_s[:, halves[h]], start=True, stop=False,
                )
        for h in range(2):
            nc.scalar.activation(
                out=hid[h][:].rearrange("p (c i) t -> p c t i", i=4),
                in_=diff[h][:].rearrange("p t (c i) -> p c t i", i=4),
                func=ACT.Abs,
            )
            nc.vector.quantize_mx(
                out=hq_w[h][:].bitcast(E4M3), scales=hq_s[h][:], in_=hid[h][:].rearrange("p j t -> p (j t)")
            )
            for g in range(2):
                nc.tensor.matmul_mx(
                    out=p_ps[h, g][:], lhsT=wb_w[:, halves[g]].bitcast(E5M2), lhsT_scale=wb_s[:, halves[g]],
                    rhs=hq_w[h][:].bitcast(E4M3), rhs_scale=hq_s[h][:], start=False, stop=True,
                )

        p0_sb = keep.tile([P, J], F32, name="p0_sb")
        p1_sb = keep.tile([P, J], F32, name="p1_sb", tag="hid1", align_bytes=64)
        nc.scalar.activation(out=p0_sb[:, halves[0]], in_=p_ps[0, 0][:], func=ACT.Copy)
        nc.scalar.activation(out=page0[:].indirect(idx5[:, 0:8]), in_=p0_sb[:, halves[0]], func=ACT.Copy)
        nc.vector.tensor_copy(out=p1_sb[:, halves[0]], in_=p_ps[0, 1][:])
        nc.vector.tensor_copy(out=p0_sb[:, halves[1]], in_=p_ps[1, 0][:])
        nc.vector.tensor_copy(out=p1_sb[:, halves[1]], in_=p_ps[1, 1][:])
        nc.scalar.activation(out=page0[:].indirect(idx5[:, 8:16]), in_=p0_sb[:, halves[1]], func=ACT.Copy)
        nc.vector.tensor_copy(out=page1[:].indirect(idx5[:]), in_=p1_sb[:])
        nc.sync.dma_start(out[0:P, :], page0[:])
        nc.sync.dma_start(out[P : 2 * P, :], page1[:])
